import numpy as np
import ml_dtypes


def mxq(x, axis, fmt="e4m3"):
    dtype, down = {"e4m3": (ml_dtypes.float8_e4m3fn, 7), "e5m2": (ml_dtypes.float8_e5m2, 14)}[fmt]
    v = np.moveaxis(np.asarray(x, np.float32).astype(ml_dtypes.bfloat16).astype(np.float64), axis, -1)
    blocks = v.reshape(v.shape[:-1] + (-1, 32))
    amax = np.abs(blocks).max(-1, keepdims=True)
    byte = np.maximum(np.where(amax > 0, np.frexp(amax)[1] - 1 + 127, 0) - down, 1)
    scale = np.exp2(byte - 127.0)
    codes = (blocks / scale).astype(np.float32).astype(dtype).astype(np.float64)
    return np.moveaxis((codes * scale).reshape(v.shape), -1, axis)


WIDE = False


def mx_kscale(k):
    if not WIDE:
        return np.ones(k)
    levels = np.array([10, -10, 5, -5, 0])
    if k % 512:
        return np.exp2(np.random.permutation(np.resize(levels, k // 32))).repeat(32)
    a = np.empty((k // 512, 16))
    for p in range(k // 512):
        a[p, :8] = np.random.permutation(np.resize(levels, 8))
        for g in range(8):
            far = levels[np.abs(levels - a[p, g]) >= 10]
            a[p, g + 8] = far[np.random.randint(len(far))]
    return np.exp2(a.ravel()).repeat(32)


def f64(x):
    return np.asarray(x).astype(np.float64)


def striped(idx):
    return np.tile(idx.reshape(-1, 16).T, (8, 1)).astype(np.uint16)


def unstriped(offs):
    return offs[:16].T.reshape(-1).astype(np.int64)


def striped8(idx):
    return np.concatenate([x.reshape(-1, 16).T for x in idx]).astype(np.uint16)


def runs(offs, k):
    lists = np.stack([offs[16 * r : 16 * r + 16].T.reshape(-1) for r in range(8)]).astype(np.int64)
    return lists[np.arange(k) % 512 // 64]


def pack_weight(w):
    k, n = w.shape
    w = f64(np.asarray(w, np.float32).astype(ml_dtypes.bfloat16)).reshape(k // 32, 32, n)
    amax = np.abs(w).max(1)
    byte = np.clip(np.where(amax > 0, np.frexp(amax)[1] - 1 + 127 - 7, 1), 1, 254)
    scaled = (w * np.exp2(127.0 - byte)[:, None, :]).reshape(k, n).astype(np.float32)
    words = np.ascontiguousarray(scaled.reshape(k // 512, 128, 4, n).transpose(0, 1, 3, 2)).astype(ml_dtypes.float8_e4m3fn).view(np.uint8)
    return words, np.ascontiguousarray(byte.astype(np.uint8).reshape(k // 512, 16, n))


def unpack_weight(words, scales):
    g, p, n, _ = words.shape
    vals = np.ascontiguousarray(words).view(ml_dtypes.float8_e4m3fn).astype(np.float64) * np.repeat(np.exp2(scales.astype(np.float64) - 127.0), 8, axis=1)[..., None]
    return vals.transpose(0, 1, 3, 2).reshape(g * 512, n)


def sigmoid(v):
    return 1.0 / (1.0 + np.exp(-np.maximum(v, -700.0)))


K, T, S, N, H, G, W = 512, 1024, 256, 512, 512, 2048, 128


def setup_inputs():
    n = np.random.standard_normal
    s = mx_kscale(K)[:, None]
    u = mx_kscale(K)
    packed_xT = pack_weight(n((K, T)) * s)
    packed_dT = pack_weight(n((K, G)) / s)
    perm = np.random.permutation(S)
    return {
        "x_words": packed_xT[0],
        "x_scales": packed_xT[1],
        "w1": (n((K, H)) / np.sqrt(K) / s).astype(np.float32),
        "d_words": packed_dT[0],
        "d_scales": packed_dT[1],
        "gn": (np.random.uniform(0.5, 1.5, (H, 1)) * u[:, None]).astype(np.float32),
        "gk": (np.random.uniform(0.5, 1.5, (H, 1)) * u[:, None]).astype(np.float32),
        "w2": (n((H, N)) / np.sqrt(2 * H) / u[:, None]).astype(np.float32),
        "w3": (n((H, N)) / np.sqrt(2 * H) / u[:, None]).astype(np.float32),
        "offs": striped(np.random.permutation(T)[:S]),
        "kidx": striped8(np.random.randint(0, G, (8, H))),
        "two": striped(np.random.permutation(T)[:S]),
        "n1": striped(np.random.permutation(S)),
        "n2": striped(np.random.permutation(S)),
        "n3": striped(np.random.permutation(S)),
        "n4": striped8(np.stack([np.random.permutation(S) for _ in range(8)])),
        "n5": striped8(np.stack([np.random.permutation(S) for _ in range(8)])),
        "n6": striped(perm[:W]),
        "n7": striped(perm[W:]),
    }


def reference(x_words, x_scales, w1, d_words, d_scales, gn, gk, w2, w3, offs, kidx, two, n1, n2, n3, n4, n5, n6, n7):
    xq = unpack_weight(x_words, x_scales)[:, unstriped(offs)]
    y = mxq(f64(w1), 0, "e4m3").T @ xq
    z = f64(gn) * (y[:, unstriped(n1)] * sigmoid(y) + y[:, unstriped(n2)] * (sigmoid(y[:, unstriped(n3)])))
    d_kidx = unpack_weight(d_words, d_scales)[np.arange(K)[:, None], runs(kidx, K)]
    x_two = unpack_weight(x_words, x_scales)[:, unstriped(two)]
    s = 0.0625 * (d_kidx.T @ x_two)
    z2 = f64(gk) * (s[np.arange(H)[:, None], runs(n4, H)] + 0.75 * (s[np.arange(H)[:, None], runs(n5, H)]))
    h = mxq(f64(w2), 0, "e4m3").T @ mxq(z, 0, "e4m3") + mxq(f64(w3), 0, "e4m3").T @ mxq(z2, 0, "e4m3")
    pa = h[:, unstriped(n6)]
    pb = h[:, unstriped(n7)]
    ra = pa * sigmoid(pb)
    out = h.copy()
    out[:, unstriped(n7)] = ra
    return out

@@ -1,0 +1,220 @@
+from contextlib import ExitStack
+
+import concourse.mybir as mybir
+
+F32 = mybir.dt.float32
+BF16 = mybir.dt.bfloat16
+I32 = mybir.dt.int32
+U32 = mybir.dt.uint32
+U16 = mybir.dt.uint16
+U8 = mybir.dt.uint8
+X4 = mybir.dt.float8_e4m3fn_x4
+ACT = mybir.ActivationFunctionType
+ALU = mybir.AluOpType
+
+K, T, S, N, H, G, W = 512, 1024, 256, 512, 512, 2048, 128
+P = 128
+PACK = 4
+SPARE = 16
+FLOPS = 4 * 2 * 512 * 512 * 256
+
+
+def tile_picked_jkeywsumsumfold_none_p_kernel(
+    tc, x_words, x_scales, w1, d_words, d_scales, gn, gk, w2, w3,
+    offs, kidx, two, n1, n2, n3, n4, n5, n6, n7, out,
+):
+    nc = tc.nc
+    with ExitStack() as ctx:
+        lists = ctx.enter_context(tc.tile_pool(name="lists", bufs=1))
+        sb = ctx.enter_context(tc.tile_pool(name="sb", bufs=1))
+        ps = ctx.enter_context(tc.psum_pool(name="ps", bufs=1))
+
+        def load_list(ap, name):
+            t = lists.tile([P, ap.shape[1]], U16, name=name)
+            nc.sync.dma_start(out=t[:], in_=ap)
+            return t
+
+        def words_of(ap):
+            return ap[0].rearrange("p n t -> p (n t)").bitcast(I32)
+
+        xs = sb.tile([P, T], U8, name="xs")
+        ds = sb.tile([P, G], U8, name="ds")
+        nc.gpsimd.memset(ds[:].bitcast(I32), 0)
+        gn_sb = sb.tile([P, PACK], F32, name="gn_sb")
+        gk_sb = sb.tile([P, PACK], F32, name="gk_sb")
+
+        l_offs = load_list(offs, "l_offs")
+        for q in range(4):
+            rows = x_scales[0][4 * q : 4 * q + 4, :].bitcast(I32)
+            nc.sync.dma_start(out=xs[32 * q : 32 * q + 32, :].bitcast(I32), in_=rows.unsqueeze(0).to_broadcast([8, 4, T // 4]))
+        l_kidx = load_list(kidx, "l_kidx")
+        nc.sync.dma_start(out=ds[0:P:8, :].bitcast(I32), in_=d_scales[0].bitcast(I32))
+        xw = sb.tile([P, T], U32, name="xw")
+        nc.sync.dma_start(out=xw[:].bitcast(I32), in_=words_of(x_words))
+        w1_raw = [sb.tile([P, PACK, H // 2], F32, name=f"w1_raw{hf}", tag=f"w1_raw{hf}") for hf in range(2)]
+        w1_rows = w1.rearrange("(p j) c -> p j c", j=PACK)
+        nc.sync.dma_start(out=w1_raw[0][:], in_=w1_rows[:, :, 0:256])
+        nc.sync.dma_start(out=w1_raw[1][:], in_=w1_rows[:, :, 256:512])
+        nc.sync.dma_start(out=gn_sb[:], in_=gn.rearrange("(p t) o -> p (t o)", t=PACK))
+        l_n3 = load_list(n3, "l_n3")
+        l_n1 = load_list(n1, "l_n1")
+        l_n2 = load_list(n2, "l_n2")
+        dw = sb.tile([P, G], U32, name="dw")
+        nc.sync.dma_start(out=dw[:].bitcast(I32), in_=words_of(d_words))
+        l_two = load_list(two, "l_two")
+        nc.sync.dma_start(out=gk_sb[:], in_=gk.rearrange("(p t) o -> p (t o)", t=PACK))
+        l_n4 = load_list(n4, "l_n4")
+        l_n5 = load_list(n5, "l_n5")
+        l_n7 = load_list(n7, "l_n7")
+        l_n6 = load_list(n6, "l_n6")
+
+        xo_s = sb.tile([P, S], U8, name="xo_s", align_bytes=64)
+        xo_w = sb.tile([P, S], U32, name="xo_w", align_bytes=64)
+        nc.vector.tensor_copy(out=xo_s[:], in_=xs[:].indirect(l_offs[:]))
+        nc.vector.tensor_copy(out=xo_w[:], in_=xw[:].indirect(l_offs[:]))
+
+        dg_s = sb.tile([P, H], U8, name="dg_s")
+        dd_s = sb.tile([P, H], U8, name="dd_s")
+        dk_s = sb.tile([P, H], U8, name="dk_s", align_bytes=64)
+        nc.gpsimd.memset(dk_s[:].bitcast(I32), 0)
+        nc.vector.tensor_copy(out=dg_s[:], in_=ds[:].indirect(l_kidx[:]))
+        nc.vector.tensor_copy(
+            out=dd_s[:].rearrange("p (t m) -> p m t", t=PACK),
+            in_=dg_s[:].rearrange("p (m t) -> p m t", t=PACK),
+        )
+        for q in range(4):
+            nc.sync.dma_start(out=dk_s[32 * q : 32 * q + 4, :].bitcast(I32), in_=dd_s[32 * q : 32 * q + 32 : 8, :].bitcast(I32))
+
+        w1_b = sb.tile([P, PACK * H], BF16, name="w1_b", align_bytes=64)
+        w1_v = w1_b[:].rearrange("p (t m j) -> p m j t", t=PACK, j=PACK)
+        for hf in range(2):
+            src = w1_raw[hf][:].rearrange("p j (m t) -> p m j t", t=PACK)
+            if hf == 0:
+                nc.scalar.copy(out=w1_v[:, 0:64], in_=src)
+            else:
+                nc.vector.tensor_copy(out=w1_v[:, 64:128], in_=src)
+        w2_raw = sb.tile([P, PACK, N], F32, name="w2_raw", tag="w1_raw1")
+        nc.sync.dma_start(out=w2_raw[:], in_=w2.rearrange("(p j) c -> p j c", j=PACK))
+        w3_raw = sb.tile([P, PACK, N], F32, name="w3_raw", tag="w1_raw0")
+        nc.sync.dma_start(out=w3_raw[:], in_=w3.rearrange("(p j) c -> p j c", j=PACK))
+        w1_w = sb.tile([P, H], U32, name="w1_w", align_bytes=64)
+        w1_s = sb.tile([P, H], U8, name="w1_s", align_bytes=64)
+
+        a_sb = sb.tile([P, PACK, S], F32, name="a_sb")
+        c_sb = sb.tile([P, PACK, S], F32, name="c_sb")
+        y_ps, y_pairs = [], []
+        for t in range(PACK):
+            cols = slice(P * t, P * t + P)
+            nc.vector.quantize_mx(out=w1_w[:, cols].bitcast(X4), scales=w1_s[:, cols], in_=w1_b[:, 512 * t : 512 * t + 512])
+            if t % 2 == 0:
+                pair = ps.tile([P, 2, S], F32, name=f"y{t // 2}")
+                y_pairs.append(pair)
+            bank = pair[:, t % 2, :]
+            nc.tensor.matmul_mx(out=bank, lhsT=w1_w[:, cols].bitcast(X4), lhsT_scale=w1_s[:, cols],
+                                rhs=xo_w[:].bitcast(X4), rhs_scale=xo_s[:], start=True, stop=True)
+            y_ps.append(bank)
+
+        xt_s = sb.tile([P, S], U8, name="xt_s", align_bytes=64)
+        xt_w = sb.tile([P, S], U32, name="xt_w", align_bytes=64)
+        nc.vector.tensor_copy(out=xt_s[:], in_=xs[:].indirect(l_two[:]))
+        nc.vector.tensor_copy(out=xt_w[:], in_=xw[:].indirect(l_two[:]))
+        dg_w = sb.tile([P, H], U32, name="dg_w")
+        dk_w = sb.tile([P, H], U32, name="dk_w", align_bytes=64)
+
+        gy = []
+        sig = sb.tile([P, (PACK + 1) * S], F32, name="sig")
+        for t in range(PACK):
+            if t % 2 == 0:
+                nc.scalar.activation(out=sig[:, S * t : S * t + 2 * S], in_=y_pairs[t // 2][:].rearrange("p a s -> p (a s)"), func=ACT.Sigmoid)
+            g = sb.tile([P, S + SPARE], F32, name=f"gy{t}")
+            nc.scalar.activation(out=g[:, 0:S], in_=y_ps[t], func=ACT.Copy, scale=gn_sb[:, t : t + 1])
+            gy.append(g)
+        for t in range(PACK):
+            nc.scalar.activation(out=c_sb[:, t, :], in_=sig[:, S * t : S * t + 2 * S].indirect(l_n3[:]), func=ACT.Copy)
+            nc.scalar.activation(out=a_sb[:, t, :], in_=gy[t][:].indirect(l_n1[:]), func=ACT.Copy)
+
+        nc.vector.tensor_copy(out=dg_w[:], in_=dw[:].indirect(l_kidx[:]))
+        nc.vector.tensor_copy(
+            out=dk_w[:].rearrange("p (t b i) -> p b t i", t=PACK, i=4),
+            in_=dg_w[:].rearrange("p (b i t) -> p b t i", t=PACK, i=4),
+        )
+        gk16 = sb.tile([P, PACK], F32, name="gk16")
+        nc.vector.tensor_scalar(out=gk16[:], in0=gk_sb[:], scalar1=0.0625, scalar2=None, op0=ALU.mult)
+        gs, s_ps = [], []
+        for t in range(PACK):
+            cols = slice(P * t, P * t + P)
+            if t % 2 == 0:
+                pair = ps.tile([P, 2, S], F32, name=f"s{t // 2}")
+            bank = pair[:, t % 2, :]
+            nc.tensor.matmul_mx(out=bank, lhsT=dk_w[:, cols].bitcast(X4), lhsT_scale=dk_s[:, cols],
+                                rhs=xt_w[:].bitcast(X4), rhs_scale=xt_s[:], start=True, stop=True)
+            s_ps.append(bank)
+        for t in range(PACK):
+            g = sb.tile([P, S], F32, name=f"gs{t}")
+            nc.scalar.activation(out=g[:], in_=s_ps[t], func=ACT.Copy, scale=gk16[:, t : t + 1])
+            gs.append(g)
+
+        def add_interleaved(dst, lhs, rhs):
+            walk = "p t (b i) -> p b t i"
+            nc.vector.tensor_tensor(out=dst[:].rearrange("p (b i t) -> p b t i", i=4, t=PACK),
+                                    in0=lhs.rearrange(walk, i=4), in1=rhs.rearrange(walk, i=4), op=ALU.add)
+
+        def quantize(name, src, width):
+            words = sb.tile([P, width], U32, name=name + "_w", align_bytes=64)
+            scales = sb.tile([P, width], U8, name=name + "_s", align_bytes=64)
+            nc.vector.quantize_mx(out=words[:].bitcast(X4), scales=scales[:], in_=src[:])
+            return words, scales
+
+        def round_weight(name, raw):
+            b = sb.tile([P, PACK * N], BF16, name=name, tag=name, align_bytes=64)
+            nc.vector.tensor_copy(out=b[:].rearrange("p (b i j) -> p b j i", i=4, j=PACK),
+                                  in_=raw[:].rearrange("p j (b i) -> p b j i", i=4))
+            return b
+
+        w2_b = round_weight("w2_b", w2_raw)
+        u_sb = w2_raw[:, :, 0:S]
+        v_sb = w2_raw[:, :, S : 2 * S]
+        for t in range(PACK):
+            nc.vector.tensor_tensor(out=v_sb[:, t, :], in0=gy[t][:].indirect(l_n2[:]), in1=c_sb[:, t, :], op=ALU.mult)
+            if t % 2 == 1:
+                nc.vector.tensor_tensor(out=u_sb[:, t - 1 : t + 1, :], in0=a_sb[:, t - 1 : t + 1, :],
+                                        in1=sig[:, S * (t - 1) : S * (t + 1)].rearrange("p (a s) -> p a s", a=2), op=ALU.mult)
+
+        w2_w, w2_s = quantize("w2", w2_b, N)
+        w3_b = round_weight("w3_b", w3_raw)
+        z_b = sb.tile([P, PACK * S], BF16, name="z_b", tag="z_b", align_bytes=64)
+        add_interleaved(z_b, u_sb, v_sb)
+        w3_w, w3_s = quantize("w3", w3_b, N)
+        z_w, z_s = quantize("z", z_b, S)
+
+        h_ps = [ps.tile([P, S], F32, name=f"h{m}") for m in range(4)]
+        h_sb = [sb.tile([P, S], F32, name=f"h_sb{m}") for m in range(4)]
+        for m in range(4):
+            cols = slice(P * m, P * m + P)
+            nc.tensor.matmul_mx(out=h_ps[m][:], lhsT=w2_w[:, cols].bitcast(X4), lhsT_scale=w2_s[:, cols],
+                                rhs=z_w[:].bitcast(X4), rhs_scale=z_s[:], start=True, stop=False)
+        for hf in range(2):
+            hc = slice(128 * hf, 128 * hf + 128)
+            lc = slice(8 * hf, 8 * hf + 8)
+            p4 = sb.tile([P, PACK, 128], F32, name=f"p4_{hf}")
+            p5 = sb.tile([P, PACK, 128], F32, name=f"p5_{hf}")
+            for t in range(PACK):
+                nc.scalar.activation(out=p4[:, t, :], in_=gs[t][:].indirect(l_n4[:, lc]), func=ACT.Copy)
+                nc.scalar.activation(out=p5[:, t, :], in_=gs[t][:].indirect(l_n5[:, lc]), func=ACT.Copy, scale=0.75)
+            z2_b = sb.tile([P, PACK * 128], BF16, name=f"z2_b{hf}", tag=("z_b", "w3_b")[hf], align_bytes=64)
+            add_interleaved(z2_b, p4[:], p5[:])
+            z2_w, z2_s = quantize(f"z2{hf}", z2_b, 128)
+            for m in range(4):
+                cols = slice(P * m, P * m + P)
+                nc.tensor.matmul_mx(out=h_ps[m][:, hc], lhsT=w3_w[:, cols].bitcast(X4), lhsT_scale=w3_s[:, cols],
+                                    rhs=z2_w[:].bitcast(X4), rhs_scale=z2_s[:], start=False, stop=(hf == 1))
+
+        for m in range(4):
+            nc.vector.tensor_copy(out=h_sb[m][:], in_=h_ps[m][:])
+        for m in range(4):
+            sgb = sb.tile([P, W], F32, name=f"sgb{m}")
+            ra = sb.tile([P, W], F32, name=f"ra{m}")
+            nc.scalar.activation(out=sgb[:], in_=h_sb[m][:].indirect(l_n7[:]), func=ACT.Sigmoid)
+            nc.vector.tensor_tensor(out=ra[:], in0=h_sb[m][:].indirect(l_n6[:]), in1=sgb[:], op=ALU.mult)
+            nc.scalar.activation(out=h_sb[m][:].indirect(l_n7[:]), in_=ra[:], func=ACT.Copy)
+            nc.sync.dma_start(out=out[P * m : P * m + P, :], in_=h_sb[m][:])

@@ -49,19 +49,20 @@ def tile_picked_jkeywsumsumfold_none_p_kernel(
             nc.sync.dma_start(out=xs[32 * q : 32 * q + 32, :].bitcast(I32), in_=rows.unsqueeze(0).to_broadcast([8, 4, T // 4]))
         l_kidx = load_list(kidx, "l_kidx")
         nc.sync.dma_start(out=ds[0:P:8, :].bitcast(I32), in_=d_scales[0].bitcast(I32))
+        w1_raw = sb.tile([P, PACK, H], F32, name="w1_raw", tag="w1_raw")
+        nc.sync.dma_start(out=w1_raw[:], in_=w1.rearrange("(p j) c -> p j c", j=PACK))
         xw = sb.tile([P, T], U32, name="xw")
         nc.sync.dma_start(out=xw[:].bitcast(I32), in_=words_of(x_words))
-        w1_raw = [sb.tile([P, PACK, H // 2], F32, name=f"w1_raw{hf}", tag=f"w1_raw{hf}") for hf in range(2)]
-        w1_rows = w1.rearrange("(p j) c -> p j c", j=PACK)
-        nc.sync.dma_start(out=w1_raw[0][:], in_=w1_rows[:, :, 0:256])
-        nc.sync.dma_start(out=w1_raw[1][:], in_=w1_rows[:, :, 256:512])
         nc.sync.dma_start(out=gn_sb[:], in_=gn.rearrange("(p t) o -> p (t o)", t=PACK))
         l_n3 = load_list(n3, "l_n3")
         l_n1 = load_list(n1, "l_n1")
         l_n2 = load_list(n2, "l_n2")
         dw = sb.tile([P, G], U32, name="dw")
-        nc.sync.dma_start(out=dw[:].bitcast(I32), in_=words_of(d_words))
+        nc.sync.dma_start(out=dw[:, 0 : G // 2].bitcast(I32), in_=words_of(d_words)[:, 0 : G // 2])
         l_two = load_list(two, "l_two")
+        nc.sync.dma_start(out=dw[:, G // 2 : G].bitcast(I32), in_=words_of(d_words)[:, G // 2 : G])
+        w2_raw = sb.tile([P, PACK, N], F32, name="w2_raw")
+        nc.sync.dma_start(out=w2_raw[:], in_=w2.rearrange("(p j) c -> p j c", j=PACK))
         nc.sync.dma_start(out=gk_sb[:], in_=gk.rearrange("(p t) o -> p (t o)", t=PACK))
         l_n4 = load_list(n4, "l_n4")
         l_n5 = load_list(n5, "l_n5")
@@ -71,7 +72,6 @@ def tile_picked_jkeywsumsumfold_none_p_kernel(
         xo_s = sb.tile([P, S], U8, name="xo_s", align_bytes=64)
         xo_w = sb.tile([P, S], U32, name="xo_w", align_bytes=64)
         nc.vector.tensor_copy(out=xo_s[:], in_=xs[:].indirect(l_offs[:]))
-        nc.vector.tensor_copy(out=xo_w[:], in_=xw[:].indirect(l_offs[:]))
 
         dg_s = sb.tile([P, H], U8, name="dg_s")
         dd_s = sb.tile([P, H], U8, name="dd_s")
@@ -85,17 +85,12 @@ def tile_picked_jkeywsumsumfold_none_p_kernel(
         for q in range(4):
             nc.sync.dma_start(out=dk_s[32 * q : 32 * q + 4, :].bitcast(I32), in_=dd_s[32 * q : 32 * q + 32 : 8, :].bitcast(I32))
 
-        w1_b = sb.tile([P, PACK * H], BF16, name="w1_b", align_bytes=64)
-        w1_v = w1_b[:].rearrange("p (t m j) -> p m j t", t=PACK, j=PACK)
-        for hf in range(2):
-            src = w1_raw[hf][:].rearrange("p j (m t) -> p m j t", t=PACK)
-            if hf == 0:
-                nc.scalar.copy(out=w1_v[:, 0:64], in_=src)
-            else:
-                nc.vector.tensor_copy(out=w1_v[:, 64:128], in_=src)
-        w2_raw = sb.tile([P, PACK, N], F32, name="w2_raw", tag="w1_raw1")
-        nc.sync.dma_start(out=w2_raw[:], in_=w2.rearrange("(p j) c -> p j c", j=PACK))
-        w3_raw = sb.tile([P, PACK, N], F32, name="w3_raw", tag="w1_raw0")
+        nc.vector.tensor_copy(out=xo_w[:], in_=xw[:].indirect(l_offs[:]))
+        w1_b = [sb.tile([P, 2 * 512], BF16, name=f"w1_b{u}", align_bytes=64) for u in range(2)]
+        w1_cols = w1_raw[:].rearrange("p j (m t) -> p m j t", t=PACK)
+        nc.vector.tensor_copy(out=w1_b[0][:].rearrange("p (t m j) -> p m j t", t=2, j=PACK), in_=w1_cols[:, :, :, 0:2])
+        nc.scalar.copy(out=w1_b[1][:].rearrange("p (t m j) -> p m j t", t=2, j=PACK), in_=w1_cols[:, :, :, 2:4])
+        w3_raw = sb.tile([P, PACK, N], F32, name="w3_raw", tag="w1_raw")
         nc.sync.dma_start(out=w3_raw[:], in_=w3.rearrange("(p j) c -> p j c", j=PACK))
         w1_w = sb.tile([P, H], U32, name="w1_w", align_bytes=64)
         w1_s = sb.tile([P, H], U8, name="w1_s", align_bytes=64)
@@ -105,9 +100,9 @@ def tile_picked_jkeywsumsumfold_none_p_kernel(
         y_ps, y_pairs = [], []
         for t in range(PACK):
             cols = slice(P * t, P * t + P)
-            nc.vector.quantize_mx(out=w1_w[:, cols].bitcast(X4), scales=w1_s[:, cols], in_=w1_b[:, 512 * t : 512 * t + 512])
+            nc.vector.quantize_mx(out=w1_w[:, cols].bitcast(X4), scales=w1_s[:, cols], in_=w1_b[t // 2][:, 512 * (t % 2) : 512 * (t % 2) + 512])
             if t % 2 == 0:
-                pair = ps.tile([P, 2, S], F32, name=f"y{t // 2}")
+                pair = ps.tile([P, 2, S], F32, name=f"y{t // 2}", tag=f"y{t // 2}")
                 y_pairs.append(pair)
             bank = pair[:, t % 2, :]
             nc.tensor.matmul_mx(out=bank, lhsT=w1_w[:, cols].bitcast(X4), lhsT_scale=w1_s[:, cols],
@@ -138,20 +133,18 @@ def tile_picked_jkeywsumsumfold_none_p_kernel(
             out=dk_w[:].rearrange("p (t b i) -> p b t i", t=PACK, i=4),
             in_=dg_w[:].rearrange("p (b i t) -> p b t i", t=PACK, i=4),
         )
-        gk16 = sb.tile([P, PACK], F32, name="gk16")
-        nc.vector.tensor_scalar(out=gk16[:], in0=gk_sb[:], scalar1=0.0625, scalar2=None, op0=ALU.mult)
         gs, s_ps = [], []
         for t in range(PACK):
             cols = slice(P * t, P * t + P)
             if t % 2 == 0:
-                pair = ps.tile([P, 2, S], F32, name=f"s{t // 2}")
+                pair = ps.tile([P, 2, S], F32, name=f"s{t // 2}", tag=f"s{t // 2}")
             bank = pair[:, t % 2, :]
             nc.tensor.matmul_mx(out=bank, lhsT=dk_w[:, cols].bitcast(X4), lhsT_scale=dk_s[:, cols],
                                 rhs=xt_w[:].bitcast(X4), rhs_scale=xt_s[:], start=True, stop=True)
             s_ps.append(bank)
         for t in range(PACK):
             g = sb.tile([P, S], F32, name=f"gs{t}")
-            nc.scalar.activation(out=g[:], in_=s_ps[t], func=ACT.Copy, scale=gk16[:, t : t + 1])
+            nc.scalar.activation(out=g[:], in_=s_ps[t], func=ACT.Copy, scale=gk_sb[:, t : t + 1])
             gs.append(g)
 
         def add_interleaved(dst, lhs, rhs):
@@ -187,34 +180,39 @@ def tile_picked_jkeywsumsumfold_none_p_kernel(
         w3_w, w3_s = quantize("w3", w3_b, N)
         z_w, z_s = quantize("z", z_b, S)
 
-        h_ps = [ps.tile([P, S], F32, name=f"h{m}") for m in range(4)]
+        h_tags = (("y0", "y1", "s0", "s1"), ("h0", "h1", "h2", "h3"))
+        h_ps = [[ps.tile([P, 128], F32, name=f"h{hf}{m}", tag=h_tags[hf][m]) for m in range(4)] for hf in range(2)]
         h_sb = [sb.tile([P, S], F32, name=f"h_sb{m}") for m in range(4)]
-        for m in range(4):
-            cols = slice(P * m, P * m + P)
-            nc.tensor.matmul_mx(out=h_ps[m][:], lhsT=w2_w[:, cols].bitcast(X4), lhsT_scale=w2_s[:, cols],
-                                rhs=z_w[:].bitcast(X4), rhs_scale=z_s[:], start=True, stop=False)
+        for hf in range(2):
+            hc = slice(128 * hf, 128 * hf + 128)
+            for m in range(4):
+                cols = slice(P * m, P * m + P)
+                nc.tensor.matmul_mx(out=h_ps[hf][m][:], lhsT=w2_w[:, cols].bitcast(X4), lhsT_scale=w2_s[:, cols],
+                                    rhs=z_w[:, hc].bitcast(X4), rhs_scale=z_s[:, hc], start=True, stop=False)
         for hf in range(2):
             hc = slice(128 * hf, 128 * hf + 128)
             lc = slice(8 * hf, 8 * hf + 8)
             p4 = sb.tile([P, PACK, 128], F32, name=f"p4_{hf}")
             p5 = sb.tile([P, PACK, 128], F32, name=f"p5_{hf}")
             for t in range(PACK):
-                nc.scalar.activation(out=p4[:, t, :], in_=gs[t][:].indirect(l_n4[:, lc]), func=ACT.Copy)
-                nc.scalar.activation(out=p5[:, t, :], in_=gs[t][:].indirect(l_n5[:, lc]), func=ACT.Copy, scale=0.75)
+                nc.scalar.activation(out=p4[:, t, :], in_=gs[t][:].indirect(l_n4[:, lc]), func=ACT.Copy, scale=0.0625)
+                nc.scalar.activation(out=p5[:, t, :], in_=gs[t][:].indirect(l_n5[:, lc]), func=ACT.Copy, scale=0.0625 * 0.75)
             z2_b = sb.tile([P, PACK * 128], BF16, name=f"z2_b{hf}", tag=("z_b", "w3_b")[hf], align_bytes=64)
             add_interleaved(z2_b, p4[:], p5[:])
             z2_w, z2_s = quantize(f"z2{hf}", z2_b, 128)
             for m in range(4):
                 cols = slice(P * m, P * m + P)
-                nc.tensor.matmul_mx(out=h_ps[m][:, hc], lhsT=w3_w[:, cols].bitcast(X4), lhsT_scale=w3_s[:, cols],
-                                    rhs=z2_w[:].bitcast(X4), rhs_scale=z2_s[:], start=False, stop=(hf == 1))
+                nc.tensor.matmul_mx(out=h_ps[hf][m][:], lhsT=w3_w[:, cols].bitcast(X4), lhsT_scale=w3_s[:, cols],
+                                    rhs=z2_w[:].bitcast(X4), rhs_scale=z2_s[:], start=False, stop=True)
+                if hf == 0:
+                    nc.scalar.copy(out=h_sb[m][:, hc], in_=h_ps[hf][m][:])
+                else:
+                    nc.vector.tensor_copy(out=h_sb[m][:, hc], in_=h_ps[hf][m][:])
 
-        for m in range(4):
-            nc.vector.tensor_copy(out=h_sb[m][:], in_=h_ps[m][:])
         for m in range(4):
             sgb = sb.tile([P, W], F32, name=f"sgb{m}")
             ra = sb.tile([P, W], F32, name=f"ra{m}")
             nc.scalar.activation(out=sgb[:], in_=h_sb[m][:].indirect(l_n7[:]), func=ACT.Sigmoid)
             nc.vector.tensor_tensor(out=ra[:], in0=h_sb[m][:].indirect(l_n6[:]), in1=sgb[:], op=ALU.mult)
             nc.scalar.activation(out=h_sb[m][:].indirect(l_n7[:]), in_=ra[:], func=ACT.Copy)
-            nc.sync.dma_start(out=out[P * m : P * m + P, :], in_=h_sb[m][:])
+            (nc.scalar if m == 3 else nc.sync).dma_start(out=out[P * m : P * m + P, :], in_=h_sb[m][:])

from contextlib import ExitStack

import concourse.mybir as mybir

F32 = mybir.dt.float32
BF16 = mybir.dt.bfloat16
I32 = mybir.dt.int32
U32 = mybir.dt.uint32
U16 = mybir.dt.uint16
U8 = mybir.dt.uint8
X4 = mybir.dt.float8_e4m3fn_x4
ACT = mybir.ActivationFunctionType
ALU = mybir.AluOpType

K, T, S, N, H, G, W = 512, 1024, 256, 512, 512, 2048, 128
P = 128
PACK = 4
SPARE = 16
FLOPS = 4 * 2 * 512 * 512 * 256


def tile_picked_jkeywsumsumfold_none_p_kernel(
    tc, x_words, x_scales, w1, d_words, d_scales, gn, gk, w2, w3,
    offs, kidx, two, n1, n2, n3, n4, n5, n6, n7, out,
):
    nc = tc.nc
    with ExitStack() as ctx:
        lists = ctx.enter_context(tc.tile_pool(name="lists", bufs=1))
        sb = ctx.enter_context(tc.tile_pool(name="sb", bufs=1))
        ps = ctx.enter_context(tc.psum_pool(name="ps", bufs=1))

        def load_list(ap, name):
            t = lists.tile([P, ap.shape[1]], U16, name=name)
            nc.sync.dma_start(out=t[:], in_=ap)
            return t

        def words_of(ap):
            return ap[0].rearrange("p n t -> p (n t)").bitcast(I32)

        xs = sb.tile([P, T], U8, name="xs")
        ds = sb.tile([P, G], U8, name="ds")
        nc.gpsimd.memset(ds[:].bitcast(I32), 0)
        gn_sb = sb.tile([P, PACK], F32, name="gn_sb")
        gk_sb = sb.tile([P, PACK], F32, name="gk_sb")

        l_offs = load_list(offs, "l_offs")
        for q in range(4):
            rows = x_scales[0][4 * q : 4 * q + 4, :].bitcast(I32)
            nc.sync.dma_start(out=xs[32 * q : 32 * q + 32, :].bitcast(I32), in_=rows.unsqueeze(0).to_broadcast([8, 4, T // 4]))
        l_kidx = load_list(kidx, "l_kidx")
        nc.sync.dma_start(out=ds[0:P:8, :].bitcast(I32), in_=d_scales[0].bitcast(I32))
        w1_raw = sb.tile([P, PACK, H], F32, name="w1_raw", tag="w1_raw")
        nc.sync.dma_start(out=w1_raw[:], in_=w1.rearrange("(p j) c -> p j c", j=PACK))
        xw = sb.tile([P, T], U32, name="xw")
        nc.sync.dma_start(out=xw[:].bitcast(I32), in_=words_of(x_words))
        nc.sync.dma_start(out=gn_sb[:], in_=gn.rearrange("(p t) o -> p (t o)", t=PACK))
        l_n3 = load_list(n3, "l_n3")
        l_n1 = load_list(n1, "l_n1")
        l_n2 = load_list(n2, "l_n2")
        dw = sb.tile([P, G], U32, name="dw")
        nc.sync.dma_start(out=dw[:, 0 : G // 2].bitcast(I32), in_=words_of(d_words)[:, 0 : G // 2])
        l_two = load_list(two, "l_two")
        nc.sync.dma_start(out=dw[:, G // 2 : G].bitcast(I32), in_=words_of(d_words)[:, G // 2 : G])
        w2_raw = sb.tile([P, PACK, N], F32, name="w2_raw")
        nc.sync.dma_start(out=w2_raw[:], in_=w2.rearrange("(p j) c -> p j c", j=PACK))
        nc.sync.dma_start(out=gk_sb[:], in_=gk.rearrange("(p t) o -> p (t o)", t=PACK))
        l_n4 = load_list(n4, "l_n4")
        l_n5 = load_list(n5, "l_n5")
        l_n7 = load_list(n7, "l_n7")
        l_n6 = load_list(n6, "l_n6")

        xo_s = sb.tile([P, S], U8, name="xo_s", align_bytes=64)
        xo_w = sb.tile([P, S], U32, name="xo_w", align_bytes=64)
        nc.vector.tensor_copy(out=xo_s[:], in_=xs[:].indirect(l_offs[:]))

        dg_s = sb.tile([P, H], U8, name="dg_s")
        dd_s = sb.tile([P, H], U8, name="dd_s")
        dk_s = sb.tile([P, H], U8, name="dk_s", align_bytes=64)
        nc.gpsimd.memset(dk_s[:].bitcast(I32), 0)
        nc.vector.tensor_copy(out=dg_s[:], in_=ds[:].indirect(l_kidx[:]))
        nc.vector.tensor_copy(
            out=dd_s[:].rearrange("p (t m) -> p m t", t=PACK),
            in_=dg_s[:].rearrange("p (m t) -> p m t", t=PACK),
        )
        for q in range(4):
            nc.sync.dma_start(out=dk_s[32 * q : 32 * q + 4, :].bitcast(I32), in_=dd_s[32 * q : 32 * q + 32 : 8, :].bitcast(I32))

        nc.vector.tensor_copy(out=xo_w[:], in_=xw[:].indirect(l_offs[:]))
        w1_b = [sb.tile([P, 2 * 512], BF16, name=f"w1_b{u}", align_bytes=64) for u in range(2)]
        w1_cols = w1_raw[:].rearrange("p j (m t) -> p m j t", t=PACK)
        nc.vector.tensor_copy(out=w1_b[0][:].rearrange("p (t m j) -> p m j t", t=2, j=PACK), in_=w1_cols[:, :, :, 0:2])
        nc.scalar.copy(out=w1_b[1][:].rearrange("p (t m j) -> p m j t", t=2, j=PACK), in_=w1_cols[:, :, :, 2:4])
        w3_raw = sb.tile([P, PACK, N], F32, name="w3_raw", tag="w1_raw")
        nc.sync.dma_start(out=w3_raw[:], in_=w3.rearrange("(p j) c -> p j c", j=PACK))
        w1_w = sb.tile([P, H], U32, name="w1_w", align_bytes=64)
        w1_s = sb.tile([P, H], U8, name="w1_s", align_bytes=64)

        a_sb = sb.tile([P, PACK, S], F32, name="a_sb")
        c_sb = sb.tile([P, PACK, S], F32, name="c_sb")
        y_ps, y_pairs = [], []
        for t in range(PACK):
            cols = slice(P * t, P * t + P)
            nc.vector.quantize_mx(out=w1_w[:, cols].bitcast(X4), scales=w1_s[:, cols], in_=w1_b[t // 2][:, 512 * (t % 2) : 512 * (t % 2) + 512])
            if t % 2 == 0:
                pair = ps.tile([P, 2, S], F32, name=f"y{t // 2}", tag=f"y{t // 2}")
                y_pairs.append(pair)
            bank = pair[:, t % 2, :]
            nc.tensor.matmul_mx(out=bank, lhsT=w1_w[:, cols].bitcast(X4), lhsT_scale=w1_s[:, cols],
                                rhs=xo_w[:].bitcast(X4), rhs_scale=xo_s[:], start=True, stop=True)
            y_ps.append(bank)

        xt_s = sb.tile([P, S], U8, name="xt_s", align_bytes=64)
        xt_w = sb.tile([P, S], U32, name="xt_w", align_bytes=64)
        nc.vector.tensor_copy(out=xt_s[:], in_=xs[:].indirect(l_two[:]))
        nc.vector.tensor_copy(out=xt_w[:], in_=xw[:].indirect(l_two[:]))
        dg_w = sb.tile([P, H], U32, name="dg_w")
        dk_w = sb.tile([P, H], U32, name="dk_w", align_bytes=64)

        gy = []
        sig = sb.tile([P, (PACK + 1) * S], F32, name="sig")
        for t in range(PACK):
            if t % 2 == 0:
                nc.scalar.activation(out=sig[:, S * t : S * t + 2 * S], in_=y_pairs[t // 2][:].rearrange("p a s -> p (a s)"), func=ACT.Sigmoid)
            g = sb.tile([P, S + SPARE], F32, name=f"gy{t}")
            nc.scalar.activation(out=g[:, 0:S], in_=y_ps[t], func=ACT.Copy, scale=gn_sb[:, t : t + 1])
            gy.append(g)
        for t in range(PACK):
            nc.scalar.activation(out=c_sb[:, t, :], in_=sig[:, S * t : S * t + 2 * S].indirect(l_n3[:]), func=ACT.Copy)
            nc.scalar.activation(out=a_sb[:, t, :], in_=gy[t][:].indirect(l_n1[:]), func=ACT.Copy)

        nc.vector.tensor_copy(out=dg_w[:], in_=dw[:].indirect(l_kidx[:]))
        nc.vector.tensor_copy(
            out=dk_w[:].rearrange("p (t b i) -> p b t i", t=PACK, i=4),
            in_=dg_w[:].rearrange("p (b i t) -> p b t i", t=PACK, i=4),
        )
        gs, s_ps = [], []
        for t in range(PACK):
            cols = slice(P * t, P * t + P)
            if t % 2 == 0:
                pair = ps.tile([P, 2, S], F32, name=f"s{t // 2}", tag=f"s{t // 2}")
            bank = pair[:, t % 2, :]
            nc.tensor.matmul_mx(out=bank, lhsT=dk_w[:, cols].bitcast(X4), lhsT_scale=dk_s[:, cols],
                                rhs=xt_w[:].bitcast(X4), rhs_scale=xt_s[:], start=True, stop=True)
            s_ps.append(bank)
        for t in range(PACK):
            g = sb.tile([P, S], F32, name=f"gs{t}")
            nc.scalar.activation(out=g[:], in_=s_ps[t], func=ACT.Copy, scale=gk_sb[:, t : t + 1])
            gs.append(g)

        def add_interleaved(dst, lhs, rhs):
            walk = "p t (b i) -> p b t i"
            nc.vector.tensor_tensor(out=dst[:].rearrange("p (b i t) -> p b t i", i=4, t=PACK),
                                    in0=lhs.rearrange(walk, i=4), in1=rhs.rearrange(walk, i=4), op=ALU.add)

        def quantize(name, src, width):
            words = sb.tile([P, width], U32, name=name + "_w", align_bytes=64)
            scales = sb.tile([P, width], U8, name=name + "_s", align_bytes=64)
            nc.vector.quantize_mx(out=words[:].bitcast(X4), scales=scales[:], in_=src[:])
            return words, scales

        def round_weight(name, raw):
            b = sb.tile([P, PACK * N], BF16, name=name, tag=name, align_bytes=64)
            nc.vector.tensor_copy(out=b[:].rearrange("p (b i j) -> p b j i", i=4, j=PACK),
                                  in_=raw[:].rearrange("p j (b i) -> p b j i", i=4))
            return b

        w2_b = round_weight("w2_b", w2_raw)
        u_sb = w2_raw[:, :, 0:S]
        v_sb = w2_raw[:, :, S : 2 * S]
        for t in range(PACK):
            nc.vector.tensor_tensor(out=v_sb[:, t, :], in0=gy[t][:].indirect(l_n2[:]), in1=c_sb[:, t, :], op=ALU.mult)
            if t % 2 == 1:
                nc.vector.tensor_tensor(out=u_sb[:, t - 1 : t + 1, :], in0=a_sb[:, t - 1 : t + 1, :],
                                        in1=sig[:, S * (t - 1) : S * (t + 1)].rearrange("p (a s) -> p a s", a=2), op=ALU.mult)

        w2_w, w2_s = quantize("w2", w2_b, N)
        w3_b = round_weight("w3_b", w3_raw)
        z_b = sb.tile([P, PACK * S], BF16, name="z_b", tag="z_b", align_bytes=64)
        add_interleaved(z_b, u_sb, v_sb)
        w3_w, w3_s = quantize("w3", w3_b, N)
        z_w, z_s = quantize("z", z_b, S)

        h_tags = (("y0", "y1", "s0", "s1"), ("h0", "h1", "h2", "h3"))
        h_ps = [[ps.tile([P, 128], F32, name=f"h{hf}{m}", tag=h_tags[hf][m]) for m in range(4)] for hf in range(2)]
        h_sb = [sb.tile([P, S], F32, name=f"h_sb{m}") for m in range(4)]
        for hf in range(2):
            hc = slice(128 * hf, 128 * hf + 128)
            for m in range(4):
                cols = slice(P * m, P * m + P)
                nc.tensor.matmul_mx(out=h_ps[hf][m][:], lhsT=w2_w[:, cols].bitcast(X4), lhsT_scale=w2_s[:, cols],
                                    rhs=z_w[:, hc].bitcast(X4), rhs_scale=z_s[:, hc], start=True, stop=False)
        for hf in range(2):
            hc = slice(128 * hf, 128 * hf + 128)
            lc = slice(8 * hf, 8 * hf + 8)
            p4 = sb.tile([P, PACK, 128], F32, name=f"p4_{hf}")
            p5 = sb.tile([P, PACK, 128], F32, name=f"p5_{hf}")
            for t in range(PACK):
                nc.scalar.activation(out=p4[:, t, :], in_=gs[t][:].indirect(l_n4[:, lc]), func=ACT.Copy, scale=0.0625)
                nc.scalar.activation(out=p5[:, t, :], in_=gs[t][:].indirect(l_n5[:, lc]), func=ACT.Copy, scale=0.0625 * 0.75)
            z2_b = sb.tile([P, PACK * 128], BF16, name=f"z2_b{hf}", tag=("z_b", "w3_b")[hf], align_bytes=64)
            add_interleaved(z2_b, p4[:], p5[:])
            z2_w, z2_s = quantize(f"z2{hf}", z2_b, 128)
            for m in range(4):
                cols = slice(P * m, P * m + P)
                nc.tensor.matmul_mx(out=h_ps[hf][m][:], lhsT=w3_w[:, cols].bitcast(X4), lhsT_scale=w3_s[:, cols],
                                    rhs=z2_w[:].bitcast(X4), rhs_scale=z2_s[:], start=False, stop=True)
                if hf == 0:
                    nc.scalar.copy(out=h_sb[m][:, hc], in_=h_ps[hf][m][:])
                else:
                    nc.vector.tensor_copy(out=h_sb[m][:, hc], in_=h_ps[hf][m][:])

        for m in range(4):
            sgb = sb.tile([P, W], F32, name=f"sgb{m}")
            ra = sb.tile([P, W], F32, name=f"ra{m}")
            nc.scalar.activation(out=sgb[:], in_=h_sb[m][:].indirect(l_n7[:]), func=ACT.Sigmoid)
            nc.vector.tensor_tensor(out=ra[:], in0=h_sb[m][:].indirect(l_n6[:]), in1=sgb[:], op=ALU.mult)
            nc.scalar.activation(out=h_sb[m][:].indirect(l_n7[:]), in_=ra[:], func=ACT.Copy)
            (nc.scalar if m == 3 else nc.sync).dma_start(out=out[P * m : P * m + P, :], in_=h_sb[m][:])
